import numpy as np
import ml_dtypes


def mxq(x, axis, fmt="e4m3"):
    dtype, down = {"e4m3": (ml_dtypes.float8_e4m3fn, 7), "e5m2": (ml_dtypes.float8_e5m2, 14)}[fmt]
    v = np.moveaxis(np.asarray(x, np.float32).astype(ml_dtypes.bfloat16).astype(np.float64), axis, -1)
    blocks = v.reshape(v.shape[:-1] + (-1, 32))
    amax = np.abs(blocks).max(-1, keepdims=True)
    byte = np.maximum(np.where(amax > 0, np.frexp(amax)[1] - 1 + 127, 0) - down, 1)
    scale = np.exp2(byte - 127.0)
    codes = (blocks / scale).astype(np.float32).astype(dtype).astype(np.float64)
    return np.moveaxis((codes * scale).reshape(v.shape), -1, axis)


WIDE = False


def mx_kscale(k):
    if not WIDE:
        return np.ones(k)
    levels = np.array([10, -10, 5, -5, 0])
    if k % 512:
        return np.exp2(np.random.permutation(np.resize(levels, k // 32))).repeat(32)
    a = np.empty((k // 512, 16))
    for p in range(k // 512):
        a[p, :8] = np.random.permutation(np.resize(levels, 8))
        for g in range(8):
            far = levels[np.abs(levels - a[p, g]) >= 10]
            a[p, g + 8] = far[np.random.randint(len(far))]
    return np.exp2(a.ravel()).repeat(32)


def f64(x):
    return np.asarray(x).astype(np.float64)


def striped(idx):
    return np.tile(idx.reshape(-1, 16).T, (8, 1)).astype(np.uint16)


def unstriped(offs):
    return offs[:16].T.reshape(-1).astype(np.int64)


def pack_weight(w):
    k, n = w.shape
    w = f64(np.asarray(w, np.float32).astype(ml_dtypes.bfloat16)).reshape(k // 32, 32, n)
    amax = np.abs(w).max(1)
    byte = np.clip(np.where(amax > 0, np.frexp(amax)[1] - 1 + 127 - 7, 1), 1, 254)
    scaled = (w * np.exp2(127.0 - byte)[:, None, :]).reshape(k, n).astype(np.float32)
    words = np.ascontiguousarray(scaled.reshape(k // 512, 128, 4, n).transpose(0, 1, 3, 2)).astype(ml_dtypes.float8_e4m3fn).view(np.uint8)
    return words, np.ascontiguousarray(byte.astype(np.uint8).reshape(k // 512, 16, n))


def unpack_weight(words, scales):
    g, p, n, _ = words.shape
    vals = np.ascontiguousarray(words).view(ml_dtypes.float8_e4m3fn).astype(np.float64) * np.repeat(np.exp2(scales.astype(np.float64) - 127.0), 8, axis=1)[..., None]
    return vals.transpose(0, 1, 3, 2).reshape(g * 512, n)


K, T, S, N, D = 1024, 1024, 512, 256, 3
P = 2 ** 7


def setup_inputs():
    n = np.random.standard_normal
    s = mx_kscale(K)[:, None]
    packed_xT = pack_weight(n((K, T)) * s)
    return {
        "x_words": packed_xT[0],
        "x_scales": packed_xT[1],
        "w1": (n((K, N)) / np.sqrt(K) / s).astype(np.float32),
        "geo": (np.tile(np.random.uniform(0.05, 0.5, (D, 1, S)), (1, P, 1))).astype(np.float32),
        "thr": (np.tile(np.random.uniform(0.5, 0.9, S), (P, 1))).astype(np.float32),
        "rated": (np.tile(np.random.uniform(0.8, 1.6, S), (P, 1))).astype(np.float32),
        "fat": (np.random.uniform(0.2, 1.0, (N, 1))).astype(np.float32),
        "offs": striped(np.random.permutation(T)[:S]),
        "pos1": striped(np.random.permutation(S)[:S]),
        "pos2": striped(np.random.permutation(S)[:S]),
        "pos3": striped(np.random.permutation(S)[:S]),
    }


def reference(x_words, x_scales, w1, geo, thr, rated, fat, offs, pos1, pos2, pos3):
    xq = unpack_weight(x_words, x_scales)[:, unstriped(offs)]
    y = mxq(f64(w1), 0, "e4m3").T @ xq
    free = 0.6 * (np.log(np.exp(y) + 1.0)) + 0.5
    cta = f64(thr)[:1] / (0.5 * free + 0.6)
    ua = free * (-1.0 * (np.sqrt((cta[:, unstriped(pos1)] * f64(geo)[0, :1]) ** 2 + (cta[:, unstriped(pos2)] * f64(geo)[1, :1]) ** 2 + (cta[:, unstriped(pos3)] * f64(geo)[2, :1]) ** 2 + 0.0004)) + 1.0)
    return (np.minimum(((ua) ** 2) * ua, f64(rated)[:1])) / (np.minimum(((free) ** 2) * free, f64(rated)[:1]) + 0.1) - (f64(fat) * ((-1.0 * (ua / free) + 1.0) ** 2))

@@ -1,0 +1,251 @@
+from contextlib import ExitStack
+
+import concourse.mybir as mybir
+from concourse.masks import make_identity
+
+K, T, S, N, D = 1024, 1024, 512, 256, 3
+FLOPS = 2 * K * S * N
+
+F32 = mybir.dt.float32
+BF16 = mybir.dt.bfloat16
+I32 = mybir.dt.int32
+U32 = mybir.dt.uint32
+U16 = mybir.dt.uint16
+U8 = mybir.dt.uint8
+FP8X4 = mybir.dt.float8_e4m3fn_x4
+ACT = mybir.ActivationFunctionType
+ALU = mybir.AluOpType
+
+P = 128
+PACK = 4
+PASSES = K // (P * PACK)
+JT = S // P
+UNITS = N // P
+SPARE = 32
+
+EXP_CAP = 2.0**60
+THR_FLOOR = 1e-15
+CUBE = 0.6**3
+SHIFT = 0.5 / 0.6
+
+
+def tile_picked_ywakef_eff_p_kernel(
+    tc, x_words, x_scales, w1, geo, thr, rated, fat, offs, pos1, pos2, pos3, out
+):
+    nc = tc.nc
+    with ExitStack() as ctx:
+        lists = ctx.enter_context(tc.tile_pool(name="lists", bufs=1))
+        sb = ctx.enter_context(tc.tile_pool(name="sb", bufs=1))
+        ps = ctx.enter_context(tc.psum_pool(name="ps", bufs=1))
+
+        words = [sb.tile([P, T], I32, name=f"words{o}", align_bytes=64) for o in range(PASSES)]
+        planes = sb.tile([P, T], U8, name="planes", align_bytes=64)
+        offs_t = lists.tile([P, S // 16], U16, name="offs_t")
+        pos_t = [lists.tile([P, S // 16], U16, name=f"pos_t{d}") for d in range(D)]
+        w_raw = [[sb.tile([P, PACK, P], F32, name=f"w_raw{u}{o}") for o in range(PASSES)] for u in range(UNITS)]
+        rows = sb.tile([P, S], F32, name="rows")
+        geo_t = [sb.tile([P, S], F32, name=f"geo_t{d}") for d in range(D)]
+        fat_row = sb.tile([P, N], F32, name="fat_row")
+        ident = sb.tile([P, P], F32, name="ident")
+        windows = [sb.tile([P, S + SPARE], F32, name=f"window{u}") for u in range(UNITS)]
+
+        nc.gpsimd.memset(planes[:].bitcast(I32), 0)
+        nc.gpsimd.memset(rows[:], 0.0)
+        make_identity(nc, ident[:])
+        for u in range(UNITS):
+            nc.gpsimd.memset(windows[u][:, S:], 0.0)
+
+        def load_words(o):
+            nc.sync.dma_start(words[o][:], x_words[o].rearrange("p n t -> p (n t)").bitcast(I32))
+
+        load_words(0)
+        nc.sync.dma_start(offs_t[:], offs)
+        for q in range(4):
+            nc.sync.dma_start(
+                planes[32 * q : 32 * q + 4 * PASSES, :].bitcast(I32),
+                x_scales[:, 4 * q : 4 * q + 4, :].bitcast(I32),
+            )
+        for o in range(PASSES):
+            if o > 0:
+                load_words(o)
+            for u in range(UNITS):
+                w_rows = w1[o * P * PACK : (o + 1) * P * PACK, u * P : (u + 1) * P]
+                nc.sync.dma_start(w_raw[u][o][:], w_rows.rearrange("(p t) m -> p t m", t=PACK))
+        for d in range(D):
+            nc.sync.dma_start(geo_t[d][:], geo[d])
+        nc.sync.dma_start(rows[0:1, :], thr[0:1, :])
+        nc.sync.dma_start(rows[1:2, :], rated[0:1, :])
+        for d, pos in enumerate((pos1, pos2, pos3)):
+            nc.sync.dma_start(pos_t[d][:], pos)
+        nc.sync.dma_start(fat_row[:], fat.rearrange("m o -> (m o)").partition_broadcast(P))
+
+        picked = [sb.tile([P, S], U32, name=f"picked{o}", align_bytes=64) for o in range(PASSES)]
+        picked_planes = sb.tile([P, S], U8, name="picked_planes", align_bytes=64)
+        expy = sb.tile([P, JT, UNITS, P], F32, name="expy")
+        y = [ps.tile([P, JT, P], F32, name=f"y{u}") for u in range(UNITS)]
+        for o in range(PASSES):
+            nc.vector.tensor_copy(picked[o][:], words[o][:].bitcast(U32).indirect(offs_t[:]))
+            if o == 0:
+                nc.vector.tensor_copy(picked_planes[:], planes[:].indirect(offs_t[:]))
+            for u in range(UNITS):
+                grouped = sb.tile([P, P, PACK], BF16, name=f"grouped{u}{o}", align_bytes=64)
+                nc.scalar.activation(
+                    grouped[:].rearrange("p (c i) t -> p c t i", i=4),
+                    w_raw[u][o][:].rearrange("p t (c i) -> p c t i", i=4),
+                    ACT.Copy,
+                )
+                w_codes = sb.tile([P, P], U32, name=f"w_codes{u}{o}", align_bytes=64)
+                w_scales = sb.tile([P, P], U8, name=f"w_scales{u}{o}", align_bytes=64)
+                nc.vector.quantize_mx(
+                    out=w_codes[:].bitcast(FP8X4),
+                    scales=w_scales[:],
+                    in_=grouped[:].rearrange("p m t -> p (m t)"),
+                )
+                for jt in range(JT):
+                    cols = slice(jt * P, (jt + 1) * P)
+                    nc.tensor.matmul_mx(
+                        out=y[u][:, jt, :],
+                        lhsT=picked[o][:, cols].bitcast(FP8X4),
+                        lhsT_scale=picked_planes[4 * o : P, cols],
+                        rhs=w_codes[:].bitcast(FP8X4),
+                        rhs_scale=w_scales[:],
+                        start=(o == 0 and jt == 0),
+                        stop=(o == PASSES - 1 and jt == JT - 1),
+                    )
+        for u in range(UNITS):
+            nc.scalar.activation(expy[:, :, u, :], y[u][:], ACT.Exp)
+
+        rows_T = ps.tile([P, JT, P], F32, name="rows_T", tag="rows_out")
+        for jt in range(JT):
+            nc.tensor.transpose(rows_T[:, jt, :], rows[:, jt * P : (jt + 1) * P], ident[:])
+        cols2 = sb.tile([P, 2, JT], F32, name="cols2")
+        nc.vector.tensor_copy(cols2[:], rows_T[:, :, 0:2].rearrange("p j r -> p r j"))
+        thr_abs = sb.tile([P, JT], F32, name="thr_abs")
+        nc.vector.scalar_tensor_tensor(thr_abs[:], cols2[:, 0, :], -1.0, cols2[:, 0, :], ALU.mult, ALU.max)
+        thr_floor = sb.tile([P, JT], F32, name="thr_floor")
+        cap = sb.tile([P, JT], F32, name="cap")
+        neg_rated = sb.tile([P, JT], F32, name="neg_rated")
+        positive = sb.tile([P, JT], F32, name="positive")
+        nc.vector.tensor_scalar(cap[:], cols2[:, 1, :], 1.0 / CUBE, -(SHIFT**3), ALU.mult, ALU.add)
+        nc.vector.tensor_scalar(thr_floor[:], thr_abs[:], THR_FLOOR, None, ALU.max)
+        nc.vector.tensor_scalar(neg_rated[:], cols2[:, 1, :], -1.0 / CUBE, None, ALU.mult)
+        nc.vector.tensor_scalar(positive[:], cols2[:, 1, :], -0.1, 2.0, ALU.is_ge, ALU.mult)
+        thr_inv = sb.tile([P, JT], F32, name="thr_inv")
+        nc.vector.reciprocal(thr_inv[:], thr_floor[:])
+        den_sign = sb.tile([P, JT], F32, name="den_sign")
+        nc.vector.tensor_scalar(den_sign[:], positive[:], -1.0, None, ALU.add)
+        den_scale = sb.tile([P, JT], F32, name="den_scale")
+        den_bias = sb.tile([P, JT], F32, name="den_bias")
+        nc.vector.tensor_scalar(den_scale[:], thr_inv[:], 0.3, None, ALU.mult)
+        nc.vector.tensor_scalar(den_bias[:], thr_inv[:], 0.85, None, ALU.mult)
+
+        capped = sb.tile([P, JT, UNITS, P], F32, name="capped")
+        log1p = sb.tile([P, JT, UNITS, P], F32, name="log1p")
+        sp = sb.tile([P, JT, UNITS, P], F32, name="sp")
+        halves = [slice(0, JT // 2), slice(JT // 2, JT)]
+        for h in halves:
+            nc.vector.tensor_scalar(capped[:, h], expy[:, h], EXP_CAP, None, ALU.min)
+        geo_sq = [sb.tile([P, S], F32, name=f"geo_sq{d}") for d in range(D)]
+        for d in range(D):
+            nc.vector.tensor_tensor(geo_sq[d][:], geo_t[d][:], geo_t[d][:], ALU.mult)
+        for h in halves:
+            nc.scalar.activation(log1p[:, h], capped[:, h], ACT.Ln, bias=1.0)
+        for h in halves:
+            for u in range(UNITS):
+                nc.vector.tensor_tensor(sp[:, h, u, :], y[u][:, h, :], log1p[:, h, u, :], ALU.max)
+        den = sb.tile([P, JT, UNITS, P], F32, name="den")
+        for jt in range(JT):
+            nc.vector.tensor_scalar(
+                den[:, jt], sp[:, jt], den_scale[:, jt : jt + 1], den_bias[:, jt : jt + 1], ALU.mult, ALU.add
+            )
+        root_T = []
+        for u in range(UNITS):
+            root = sb.tile([P, JT, P], F32, name=f"root{u}")
+            root_ps = ps.tile([P, JT, P], F32, name=f"root_ps{u}")
+            nc.scalar.activation(root[:], den[:, :, u, :], ACT.Abs_reciprocal_sqrt)
+            for jt in range(JT):
+                nc.tensor.transpose(root_ps[:, jt, :], root[:, jt, :], ident[:])
+            root_T.append(root_ps)
+        for u in range(UNITS):
+            cta = sb.tile([P, S], F32, name=f"cta{u}")
+            nc.scalar.activation(cta[:], root_T[u][:].rearrange("p j m -> p (j m)"), ACT.Square)
+            nc.scalar.activation(windows[u][:, 0:S], cta[:], ACT.Square)
+
+        sp_flat = sp[:].rearrange("p j u m -> p (j u m)")
+        quad = sb.tile([P, UNITS * S], F32, name="quad")
+        cubic = sb.tile([P, JT, UNITS, P], F32, name="cubic")
+        cubic_flat = cubic[:].rearrange("p j u m -> p (j u m)")
+        nc.vector.scalar_tensor_tensor(quad[:], sp_flat, 3 * SHIFT, sp_flat, ALU.add, ALU.mult)
+        nc.vector.scalar_tensor_tensor(cubic_flat, quad[:], 3 * SHIFT**2, sp_flat, ALU.add, ALU.mult)
+        power_den = sb.tile([P, JT, UNITS, P], F32, name="power_den")
+        for jt in range(JT):
+            nc.vector.tensor_scalar(
+                power_den[:, jt], cubic[:, jt], cap[:, jt : jt + 1], SHIFT**3 + 0.1 / CUBE, ALU.min, ALU.add
+            )
+        shared = power_den[:].rearrange("p j u m -> p (j u m)")
+
+        s_T = []
+        for u in range(UNITS):
+            s_u = ps.tile([P, JT, P], F32, name=f"s_T{u}")
+            for d in range(D):
+                term = sb.tile([P, S], F32, name=f"term{u}{d}")
+                nc.vector.tensor_tensor(term[:], windows[u][:].indirect(pos_t[d][:]), geo_sq[d][:], ALU.mult)
+                for jt in range(JT):
+                    nc.tensor.matmul(
+                        s_u[:, jt, :], term[:, jt * P : (jt + 1) * P], ident[:],
+                        start=(d == 0 and jt == 0), stop=(d == D - 1 and jt == JT - 1), is_transpose=True,
+                    )
+            s_T.append(s_u)
+
+        inv_root = sb.tile([P, UNITS * S], F32, name="inv_root")
+        nc.scalar.activation(inv_root[:], shared, ACT.Abs_reciprocal_sqrt)
+        inv_abs = sb.tile([P, JT, UNITS, P], F32, name="inv_abs")
+        inv = sb.tile([P, JT, UNITS, P], F32, name="inv")
+
+        chunks = [(0, slice(0, JT), "out0"), (1, halves[0], "y0"), (1, halves[1], "y1")]
+        deficit = []
+        kept_sq = []
+        loss = []
+        for u in range(UNITS):
+            m_cols = slice(u * P, (u + 1) * P)
+            deficit_u = shared[:, u * S : (u + 1) * S]
+            nc.scalar.activation(deficit_u, s_T[u][:].rearrange("p j m -> p (j m)"), ACT.Sqrt, bias=0.0004)
+            kept_u = sb.tile([P, JT, P], F32, name=f"kept_sq{u}")
+            nc.scalar.activation(kept_u[:].rearrange("p j m -> p (j m)"), deficit_u, ACT.Square, bias=1.0, scale=-1.0)
+            if u == 0:
+                nc.scalar.activation(inv_abs[:].rearrange("p j u m -> p (j u m)"), inv_root[:], ACT.Square)
+                for jt in range(JT):
+                    nc.scalar.activation(inv[:, jt], inv_abs[:, jt], ACT.Copy, scale=den_sign[:, jt : jt + 1])
+            loss_u = sb.tile([P, JT, P], F32, name=f"loss{u}")
+            nc.vector.scalar_tensor_tensor(
+                loss_u[:], s_T[u][:], 0.0004, fat_row[:, m_cols].unsqueeze(1).to_broadcast([P, JT, P]), ALU.add, ALU.mult
+            )
+            deficit.append(deficit_u.rearrange("p (j m) -> p j m", m=P))
+            kept_sq.append(kept_u)
+            loss.append(loss_u)
+        for c, (u, js, tag) in enumerate(chunks):
+            n_j = js.stop - js.start
+            neg_kept3 = sb.tile([P, n_j, P], F32, name=f"neg_kept3{c}")
+            nc.vector.scalar_tensor_tensor(
+                neg_kept3[:], deficit[u][:, js, :], 1.0, kept_sq[u][:, js, :], ALU.subtract, ALU.mult
+            )
+            neg_ua3 = sb.tile([P, n_j, P], F32, name=f"neg_ua3{c}")
+            nc.vector.scalar_tensor_tensor(neg_ua3[:], cubic[:, js, u, :], SHIFT**3, neg_kept3[:], ALU.add, ALU.mult)
+            neg_eff = sb.tile([P, n_j, P], F32, name=f"neg_eff{c}")
+            out_ps = ps.tile([P, n_j, P], F32, name=f"out_ps{c}", tag=tag)
+            for i in range(n_j):
+                jt = js.start + i
+                nc.tensor.matmul(
+                    out_ps[:, i, :], loss[u][:, jt, :], ident[:], start=(i == 0), stop=False, is_transpose=True
+                )
+            for i in range(n_j):
+                jt = js.start + i
+                nc.vector.scalar_tensor_tensor(
+                    neg_eff[:, i, :], neg_ua3[:, i, :], neg_rated[:, jt : jt + 1], inv[:, jt, u, :], ALU.max, ALU.mult
+                )
+                nc.tensor.matmul(
+                    out_ps[:, i, :], neg_eff[:, i, :], ident[:], start=False, stop=(i == n_j - 1), is_transpose=True
+                )
+            result = sb.tile([P, n_j * P], F32, name=f"result{c}")
+            nc.scalar.activation(result[:], out_ps[:].rearrange("p j m -> p (j m)"), ACT.Copy, scale=-1.0)
+            nc.sync.dma_start(out[u * P : (u + 1) * P, js.start * P : js.stop * P], result[:])

@@ -1,3 +1,4 @@
+import math
 from contextlib import ExitStack
 
 import concourse.mybir as mybir
@@ -24,7 +25,7 @@ UNITS = N // P
 SPARE = 32
 
 EXP_CAP = 2.0**60
-THR_FLOOR = 1e-15
+THR_FLOOR = 1e-30
 CUBE = 0.6**3
 SHIFT = 0.5 / 0.6
 
@@ -38,126 +39,143 @@ def tile_picked_ywakef_eff_p_kernel(
         sb = ctx.enter_context(tc.tile_pool(name="sb", bufs=1))
         ps = ctx.enter_context(tc.psum_pool(name="ps", bufs=1))
 
-        words = [sb.tile([P, T], I32, name=f"words{o}", align_bytes=64) for o in range(PASSES)]
+        words = [sb.tile([P, T], I32, name=f"words{o}", tag=f"words{o}", align_bytes=64) for o in range(PASSES)]
         planes = sb.tile([P, T], U8, name="planes", align_bytes=64)
         offs_t = lists.tile([P, S // 16], U16, name="offs_t")
         pos_t = [lists.tile([P, S // 16], U16, name=f"pos_t{d}") for d in range(D)]
-        w_raw = [[sb.tile([P, PACK, P], F32, name=f"w_raw{u}{o}") for o in range(PASSES)] for u in range(UNITS)]
-        rows = sb.tile([P, S], F32, name="rows")
-        geo_t = [sb.tile([P, S], F32, name=f"geo_t{d}") for d in range(D)]
+        w_raw = [sb.tile([P, PACK, N], F32, name=f"w_raw{o}") for o in range(PASSES)]
+        thr_col = sb.tile([P, JT], F32, name="thr_col")
+        rated_col = sb.tile([P, JT], F32, name="rated_col")
+        geo_t = sb.tile([P, D, S], F32, name="geo_t")
         fat_row = sb.tile([P, N], F32, name="fat_row")
         ident = sb.tile([P, P], F32, name="ident")
         windows = [sb.tile([P, S + SPARE], F32, name=f"window{u}") for u in range(UNITS)]
 
         nc.gpsimd.memset(planes[:].bitcast(I32), 0)
-        nc.gpsimd.memset(rows[:], 0.0)
-        make_identity(nc, ident[:])
-        for u in range(UNITS):
-            nc.gpsimd.memset(windows[u][:, S:], 0.0)
 
         def load_words(o):
             nc.sync.dma_start(words[o][:], x_words[o].rearrange("p n t -> p (n t)").bitcast(I32))
 
-        load_words(0)
         nc.sync.dma_start(offs_t[:], offs)
+        load_words(0)
         for q in range(4):
             nc.sync.dma_start(
                 planes[32 * q : 32 * q + 4 * PASSES, :].bitcast(I32),
                 x_scales[:, 4 * q : 4 * q + 4, :].bitcast(I32),
             )
         for o in range(PASSES):
-            if o > 0:
-                load_words(o)
-            for u in range(UNITS):
-                w_rows = w1[o * P * PACK : (o + 1) * P * PACK, u * P : (u + 1) * P]
-                nc.sync.dma_start(w_raw[u][o][:], w_rows.rearrange("(p t) m -> p t m", t=PACK))
-        for d in range(D):
-            nc.sync.dma_start(geo_t[d][:], geo[d])
-        nc.sync.dma_start(rows[0:1, :], thr[0:1, :])
-        nc.sync.dma_start(rows[1:2, :], rated[0:1, :])
+            w_rows = w1[o * P * PACK : (o + 1) * P * PACK, :]
+            nc.sync.dma_start(w_raw[o][:], w_rows.rearrange("(p t) m -> p t m", t=PACK))
+        load_words(1)
+        with nc.allow_non_contiguous_dma(reason="one value a partition"):
+            nc.sync.dma_start(thr_col[:], thr[0].rearrange("(j p) -> p j", p=P))
+            nc.sync.dma_start(rated_col[:], rated[0].rearrange("(j p) -> p j", p=P))
+        nc.sync.dma_start(geo_t[:], geo.rearrange("d p s -> p d s"))
         for d, pos in enumerate((pos1, pos2, pos3)):
             nc.sync.dma_start(pos_t[d][:], pos)
         nc.sync.dma_start(fat_row[:], fat.rearrange("m o -> (m o)").partition_broadcast(P))
 
-        picked = [sb.tile([P, S], U32, name=f"picked{o}", align_bytes=64) for o in range(PASSES)]
+        make_identity(nc, ident[:])
+        for u in range(UNITS):
+            nc.gpsimd.memset(windows[u][:, S:], 0.0)
+
+        halves = [slice(0, JT // 2), slice(JT // 2, JT)]
         picked_planes = sb.tile([P, S], U8, name="picked_planes", align_bytes=64)
         expy = sb.tile([P, JT, UNITS, P], F32, name="expy")
-        y = [ps.tile([P, JT, P], F32, name=f"y{u}") for u in range(UNITS)]
-        for o in range(PASSES):
-            nc.vector.tensor_copy(picked[o][:], words[o][:].bitcast(U32).indirect(offs_t[:]))
-            if o == 0:
-                nc.vector.tensor_copy(picked_planes[:], planes[:].indirect(offs_t[:]))
-            for u in range(UNITS):
-                grouped = sb.tile([P, P, PACK], BF16, name=f"grouped{u}{o}", align_bytes=64)
-                nc.scalar.activation(
-                    grouped[:].rearrange("p (c i) t -> p c t i", i=4),
-                    w_raw[u][o][:].rearrange("p t (c i) -> p c t i", i=4),
-                    ACT.Copy,
-                )
-                w_codes = sb.tile([P, P], U32, name=f"w_codes{u}{o}", align_bytes=64)
-                w_scales = sb.tile([P, P], U8, name=f"w_scales{u}{o}", align_bytes=64)
-                nc.vector.quantize_mx(
-                    out=w_codes[:].bitcast(FP8X4),
-                    scales=w_scales[:],
-                    in_=grouped[:].rearrange("p m t -> p (m t)"),
-                )
-                for jt in range(JT):
-                    cols = slice(jt * P, (jt + 1) * P)
-                    nc.tensor.matmul_mx(
-                        out=y[u][:, jt, :],
-                        lhsT=picked[o][:, cols].bitcast(FP8X4),
-                        lhsT_scale=picked_planes[4 * o : P, cols],
-                        rhs=w_codes[:].bitcast(FP8X4),
-                        rhs_scale=w_scales[:],
-                        start=(o == 0 and jt == 0),
-                        stop=(o == PASSES - 1 and jt == JT - 1),
-                    )
-        for u in range(UNITS):
-            nc.scalar.activation(expy[:, :, u, :], y[u][:], ACT.Exp)
+        y = [ps.tile([P, JT // 2, N], F32, name=f"y{h}") for h in range(2)]
 
-        rows_T = ps.tile([P, JT, P], F32, name="rows_T", tag="rows_out")
-        for jt in range(JT):
-            nc.tensor.transpose(rows_T[:, jt, :], rows[:, jt * P : (jt + 1) * P], ident[:])
-        cols2 = sb.tile([P, 2, JT], F32, name="cols2")
-        nc.vector.tensor_copy(cols2[:], rows_T[:, :, 0:2].rearrange("p j r -> p r j"))
-        thr_abs = sb.tile([P, JT], F32, name="thr_abs")
-        nc.vector.scalar_tensor_tensor(thr_abs[:], cols2[:, 0, :], -1.0, cols2[:, 0, :], ALU.mult, ALU.max)
-        thr_floor = sb.tile([P, JT], F32, name="thr_floor")
+        def quantise(o, tag):
+            grouped = sb.tile([P, N, PACK], BF16, name=f"grouped{o}", tag=tag, align_bytes=64)
+            for u in range(UNITS):
+                m_cols = slice(u * P, (u + 1) * P)
+                dst = grouped[:, m_cols, :].rearrange("p (c i) t -> p c t i", i=4)
+                src = w_raw[o][:, :, m_cols].rearrange("p t (c i) -> p c t i", i=4)
+                if o == PASSES - 1 and u == UNITS - 1:
+                    nc.vector.tensor_copy(dst, src)
+                else:
+                    nc.scalar.activation(dst, src, ACT.Copy)
+            w_codes = sb.tile([P, N], U32, name=f"w_codes{o}", align_bytes=64)
+            w_scales = sb.tile([P, N], U8, name=f"w_scales{o}", align_bytes=64)
+            nc.vector.quantize_mx(
+                out=w_codes[:].bitcast(FP8X4), scales=w_scales[:], in_=grouped[:].rearrange("p m t -> p (m t)")
+            )
+            return w_codes, w_scales
+
+        def multiply(o, h, picked, w_codes, w_scales):
+            for i in range(JT // 2):
+                jt = halves[h].start + i
+                cols = slice(jt * P, (jt + 1) * P)
+                nc.tensor.matmul_mx(
+                    out=y[h][:, i, :],
+                    lhsT=picked[:, cols].bitcast(FP8X4),
+                    lhsT_scale=picked_planes[4 * o : P, cols],
+                    rhs=w_codes[:].bitcast(FP8X4),
+                    rhs_scale=w_scales[:],
+                    start=(o == 0 and i == 0),
+                    stop=(o == PASSES - 1 and i == JT // 2 - 1),
+                )
+
+        picked0 = sb.tile([P, S], U32, name="picked0", align_bytes=64)
+        nc.vector.tensor_copy(picked0[:], words[0][:].bitcast(U32).indirect(offs_t[:]))
+        nc.vector.tensor_copy(picked_planes[:], planes[:].indirect(offs_t[:]))
+        weights0 = quantise(0, "grouped0")
+        for h in range(2):
+            multiply(0, h, picked0, *weights0)
+        weights1 = quantise(1, "grouped1_then_picked1")
+        picked1 = sb.tile([P, S], U32, name="picked1", tag="grouped1_then_picked1", align_bytes=64)
+        for h in range(2):
+            nc.vector.tensor_copy(
+                picked1[:, h * S // 2 : (h + 1) * S // 2],
+                words[1][:].bitcast(U32).indirect(offs_t[:, h * S // 32 : (h + 1) * S // 32]),
+            )
+            multiply(1, h, picked1, *weights1)
+            nc.scalar.activation(expy[:, halves[h]].rearrange("p j u m -> p j (u m)"), y[h][:], ACT.Exp)
+
+        thr_part = sb.tile([P, JT], F32, name="thr_part")
         cap = sb.tile([P, JT], F32, name="cap")
         neg_rated = sb.tile([P, JT], F32, name="neg_rated")
         positive = sb.tile([P, JT], F32, name="positive")
-        nc.vector.tensor_scalar(cap[:], cols2[:, 1, :], 1.0 / CUBE, -(SHIFT**3), ALU.mult, ALU.add)
-        nc.vector.tensor_scalar(thr_floor[:], thr_abs[:], THR_FLOOR, None, ALU.max)
-        nc.vector.tensor_scalar(neg_rated[:], cols2[:, 1, :], -1.0 / CUBE, None, ALU.mult)
-        nc.vector.tensor_scalar(positive[:], cols2[:, 1, :], -0.1, 2.0, ALU.is_ge, ALU.mult)
-        thr_inv = sb.tile([P, JT], F32, name="thr_inv")
-        nc.vector.reciprocal(thr_inv[:], thr_floor[:])
         den_sign = sb.tile([P, JT], F32, name="den_sign")
-        nc.vector.tensor_scalar(den_sign[:], positive[:], -1.0, None, ALU.add)
-        den_scale = sb.tile([P, JT], F32, name="den_scale")
-        den_bias = sb.tile([P, JT], F32, name="den_bias")
-        nc.vector.tensor_scalar(den_scale[:], thr_inv[:], 0.3, None, ALU.mult)
-        nc.vector.tensor_scalar(den_bias[:], thr_inv[:], 0.85, None, ALU.mult)
+        den_scale = sb.tile([P, JT], F32, name="den_scale", tag="grouped1_then_picked1", align_bytes=64)
+        nc.gpsimd.tensor_scalar(thr_part[:], thr_col[:], THR_FLOOR, 1.0 / 0.3, ALU.add, ALU.mult)
+        nc.gpsimd.tensor_scalar(cap[:], rated_col[:], 1.0 / CUBE, 0.0, ALU.mult, ALU.add)
+        nc.gpsimd.tensor_scalar(neg_rated[:], rated_col[:], -1.0 / CUBE, 0.0, ALU.mult, ALU.add)
+        nc.gpsimd.tensor_scalar(positive[:], rated_col[:], -0.1, None, ALU.is_ge)
+        nc.gpsimd.tensor_scalar(den_sign[:], positive[:], 2.0, -1.0, ALU.mult, ALU.add)
+        nc.vector.reciprocal(den_scale[:], thr_part[:])
 
         capped = sb.tile([P, JT, UNITS, P], F32, name="capped")
         log1p = sb.tile([P, JT, UNITS, P], F32, name="log1p")
         sp = sb.tile([P, JT, UNITS, P], F32, name="sp")
-        halves = [slice(0, JT // 2), slice(JT // 2, JT)]
-        for h in halves:
-            nc.vector.tensor_scalar(capped[:, h], expy[:, h], EXP_CAP, None, ALU.min)
-        geo_sq = [sb.tile([P, S], F32, name=f"geo_sq{d}") for d in range(D)]
+        nc.vector.tensor_scalar(capped[:], expy[:], EXP_CAP, None, ALU.min)
+        geo_sq = sb.tile([P, D, S], F32, name="geo_sq", tag="words1", align_bytes=64)
         for d in range(D):
-            nc.vector.tensor_tensor(geo_sq[d][:], geo_t[d][:], geo_t[d][:], ALU.mult)
+            nc.vector.tensor_tensor(geo_sq[:, d, :], geo_t[:, d, :], geo_t[:, d, :], ALU.mult)
         for h in halves:
-            nc.scalar.activation(log1p[:, h], capped[:, h], ACT.Ln, bias=1.0)
-        for h in halves:
-            for u in range(UNITS):
-                nc.vector.tensor_tensor(sp[:, h, u, :], y[u][:, h, :], log1p[:, h, u, :], ALU.max)
+            nc.scalar.activation(log1p[:, h], capped[:, h], ACT.Ln, bias=math.exp(SHIFT), scale=math.exp(SHIFT))
         den = sb.tile([P, JT, UNITS, P], F32, name="den")
+        for h in range(2):
+            nc.vector.scalar_tensor_tensor(
+                sp[:, halves[h]].rearrange("p j u m -> p j (u m)"), y[h][:], SHIFT,
+                log1p[:, halves[h]].rearrange("p j u m -> p j (u m)"), ALU.add, ALU.max,
+            )
+            for jt in range(halves[h].start, halves[h].stop):
+                nc.vector.tensor_scalar(den[:, jt], sp[:, jt], 2.0, den_scale[:, jt : jt + 1], ALU.add, ALU.mult)
+        quad = sb.tile([P, JT, UNITS, P], F32, name="quad")
+        cubic = sb.tile([P, JT, UNITS, P], F32, name="cubic")
+        for h in halves:
+            nc.vector.tensor_tensor(quad[:, h], sp[:, h], sp[:, h], ALU.mult)
+        for h in halves:
+            nc.vector.tensor_tensor(cubic[:, h], quad[:, h], sp[:, h], ALU.mult)
+        power_den = sb.tile([P, JT, UNITS, P], F32, name="power_den")
         for jt in range(JT):
             nc.vector.tensor_scalar(
-                den[:, jt], sp[:, jt], den_scale[:, jt : jt + 1], den_bias[:, jt : jt + 1], ALU.mult, ALU.add
+                power_den[:, jt], cubic[:, jt], cap[:, jt : jt + 1], 0.1 / CUBE, ALU.min, ALU.add
             )
+        shared = power_den[:].rearrange("p j u m -> p (j u m)")
+
+        inv_root = sb.tile([P, JT, UNITS, P], F32, name="inv_root")
+        ctas = [inv_root[:].rearrange("p j u m -> p (j u m)")[:, 0:S], shared[:, 0:S]]
         root_T = []
         for u in range(UNITS):
             root = sb.tile([P, JT, P], F32, name=f"root{u}")
@@ -167,29 +185,17 @@ def tile_picked_ywakef_eff_p_kernel(
                 nc.tensor.transpose(root_ps[:, jt, :], root[:, jt, :], ident[:])
             root_T.append(root_ps)
         for u in range(UNITS):
-            cta = sb.tile([P, S], F32, name=f"cta{u}")
-            nc.scalar.activation(cta[:], root_T[u][:].rearrange("p j m -> p (j m)"), ACT.Square)
-            nc.scalar.activation(windows[u][:, 0:S], cta[:], ACT.Square)
-
-        sp_flat = sp[:].rearrange("p j u m -> p (j u m)")
-        quad = sb.tile([P, UNITS * S], F32, name="quad")
-        cubic = sb.tile([P, JT, UNITS, P], F32, name="cubic")
-        cubic_flat = cubic[:].rearrange("p j u m -> p (j u m)")
-        nc.vector.scalar_tensor_tensor(quad[:], sp_flat, 3 * SHIFT, sp_flat, ALU.add, ALU.mult)
-        nc.vector.scalar_tensor_tensor(cubic_flat, quad[:], 3 * SHIFT**2, sp_flat, ALU.add, ALU.mult)
-        power_den = sb.tile([P, JT, UNITS, P], F32, name="power_den")
-        for jt in range(JT):
-            nc.vector.tensor_scalar(
-                power_den[:, jt], cubic[:, jt], cap[:, jt : jt + 1], SHIFT**3 + 0.1 / CUBE, ALU.min, ALU.add
-            )
-        shared = power_den[:].rearrange("p j u m -> p (j u m)")
+            if u == UNITS - 1:
+                nc.scalar.activation(inv_root[:], power_den[:], ACT.Abs_reciprocal_sqrt)
+            nc.scalar.activation(ctas[u], root_T[u][:].rearrange("p j m -> p (j m)"), ACT.Square)
+            nc.scalar.activation(windows[u][:, 0:S], ctas[u], ACT.Square)
 
         s_T = []
         for u in range(UNITS):
             s_u = ps.tile([P, JT, P], F32, name=f"s_T{u}")
             for d in range(D):
                 term = sb.tile([P, S], F32, name=f"term{u}{d}")
-                nc.vector.tensor_tensor(term[:], windows[u][:].indirect(pos_t[d][:]), geo_sq[d][:], ALU.mult)
+                nc.vector.tensor_tensor(term[:], windows[u][:].indirect(pos_t[d][:]), geo_sq[:, d, :], ALU.mult)
                 for jt in range(JT):
                     nc.tensor.matmul(
                         s_u[:, jt, :], term[:, jt * P : (jt + 1) * P], ident[:],
@@ -197,25 +203,21 @@ def tile_picked_ywakef_eff_p_kernel(
                     )
             s_T.append(s_u)
 
-        inv_root = sb.tile([P, UNITS * S], F32, name="inv_root")
-        nc.scalar.activation(inv_root[:], shared, ACT.Abs_reciprocal_sqrt)
-        inv_abs = sb.tile([P, JT, UNITS, P], F32, name="inv_abs")
+        inv_abs = [sb.tile([P, JT, P], F32, name=f"inv_abs{u}") for u in range(UNITS)]
         inv = sb.tile([P, JT, UNITS, P], F32, name="inv")
-
         chunks = [(0, slice(0, JT), "out0"), (1, halves[0], "y0"), (1, halves[1], "y1")]
         deficit = []
         kept_sq = []
         loss = []
         for u in range(UNITS):
             m_cols = slice(u * P, (u + 1) * P)
-            deficit_u = shared[:, u * S : (u + 1) * S]
+            deficit_u = shared[:, 0:S] if u == 0 else inv_abs[0][:].rearrange("p j m -> p (j m)")
             nc.scalar.activation(deficit_u, s_T[u][:].rearrange("p j m -> p (j m)"), ACT.Sqrt, bias=0.0004)
             kept_u = sb.tile([P, JT, P], F32, name=f"kept_sq{u}")
             nc.scalar.activation(kept_u[:].rearrange("p j m -> p (j m)"), deficit_u, ACT.Square, bias=1.0, scale=-1.0)
-            if u == 0:
-                nc.scalar.activation(inv_abs[:].rearrange("p j u m -> p (j u m)"), inv_root[:], ACT.Square)
-                for jt in range(JT):
-                    nc.scalar.activation(inv[:, jt], inv_abs[:, jt], ACT.Copy, scale=den_sign[:, jt : jt + 1])
+            nc.scalar.activation(inv_abs[u][:], inv_root[:, :, u, :], ACT.Square)
+            for jt in range(JT):
+                nc.scalar.activation(inv[:, jt, u, :], inv_abs[u][:, jt, :], ACT.Copy, scale=den_sign[:, jt : jt + 1])
             loss_u = sb.tile([P, JT, P], F32, name=f"loss{u}")
             nc.vector.scalar_tensor_tensor(
                 loss_u[:], s_T[u][:], 0.0004, fat_row[:, m_cols].unsqueeze(1).to_broadcast([P, JT, P]), ALU.add, ALU.mult
@@ -230,7 +232,7 @@ def tile_picked_ywakef_eff_p_kernel(
                 neg_kept3[:], deficit[u][:, js, :], 1.0, kept_sq[u][:, js, :], ALU.subtract, ALU.mult
             )
             neg_ua3 = sb.tile([P, n_j, P], F32, name=f"neg_ua3{c}")
-            nc.vector.scalar_tensor_tensor(neg_ua3[:], cubic[:, js, u, :], SHIFT**3, neg_kept3[:], ALU.add, ALU.mult)
+            nc.vector.tensor_tensor(neg_ua3[:], cubic[:, js, u, :], neg_kept3[:], ALU.mult)
             neg_eff = sb.tile([P, n_j, P], F32, name=f"neg_eff{c}")
             out_ps = ps.tile([P, n_j, P], F32, name=f"out_ps{c}", tag=tag)
             for i in range(n_j):
@@ -248,4 +250,5 @@ def tile_picked_ywakef_eff_p_kernel(
                 )
             result = sb.tile([P, n_j * P], F32, name=f"result{c}")
             nc.scalar.activation(result[:], out_ps[:].rearrange("p j m -> p (j m)"), ACT.Copy, scale=-1.0)
-            nc.sync.dma_start(out[u * P : (u + 1) * P, js.start * P : js.stop * P], result[:])
+            queue = nc.scalar if c == len(chunks) - 1 else nc.sync
+            queue.dma_start(out[u * P : (u + 1) * P, js.start * P : js.stop * P], result[:])

import math
from contextlib import ExitStack

import concourse.mybir as mybir
from concourse.masks import make_identity

K, T, S, N, D = 1024, 1024, 512, 256, 3
FLOPS = 2 * K * S * N

F32 = mybir.dt.float32
BF16 = mybir.dt.bfloat16
I32 = mybir.dt.int32
U32 = mybir.dt.uint32
U16 = mybir.dt.uint16
U8 = mybir.dt.uint8
FP8X4 = mybir.dt.float8_e4m3fn_x4
ACT = mybir.ActivationFunctionType
ALU = mybir.AluOpType

P = 128
PACK = 4
PASSES = K // (P * PACK)
JT = S // P
UNITS = N // P
SPARE = 32

EXP_CAP = 2.0**60
THR_FLOOR = 1e-30
CUBE = 0.6**3
SHIFT = 0.5 / 0.6


def tile_picked_ywakef_eff_p_kernel(
    tc, x_words, x_scales, w1, geo, thr, rated, fat, offs, pos1, pos2, pos3, out
):
    nc = tc.nc
    with ExitStack() as ctx:
        lists = ctx.enter_context(tc.tile_pool(name="lists", bufs=1))
        sb = ctx.enter_context(tc.tile_pool(name="sb", bufs=1))
        ps = ctx.enter_context(tc.psum_pool(name="ps", bufs=1))

        words = [sb.tile([P, T], I32, name=f"words{o}", tag=f"words{o}", align_bytes=64) for o in range(PASSES)]
        planes = sb.tile([P, T], U8, name="planes", align_bytes=64)
        offs_t = lists.tile([P, S // 16], U16, name="offs_t")
        pos_t = [lists.tile([P, S // 16], U16, name=f"pos_t{d}") for d in range(D)]
        w_raw = [sb.tile([P, PACK, N], F32, name=f"w_raw{o}") for o in range(PASSES)]
        thr_col = sb.tile([P, JT], F32, name="thr_col")
        rated_col = sb.tile([P, JT], F32, name="rated_col")
        geo_t = sb.tile([P, D, S], F32, name="geo_t")
        fat_row = sb.tile([P, N], F32, name="fat_row")
        ident = sb.tile([P, P], F32, name="ident")
        windows = [sb.tile([P, S + SPARE], F32, name=f"window{u}") for u in range(UNITS)]

        nc.gpsimd.memset(planes[:].bitcast(I32), 0)

        def load_words(o):
            nc.sync.dma_start(words[o][:], x_words[o].rearrange("p n t -> p (n t)").bitcast(I32))

        nc.sync.dma_start(offs_t[:], offs)
        load_words(0)
        for q in range(4):
            nc.sync.dma_start(
                planes[32 * q : 32 * q + 4 * PASSES, :].bitcast(I32),
                x_scales[:, 4 * q : 4 * q + 4, :].bitcast(I32),
            )
        for o in range(PASSES):
            w_rows = w1[o * P * PACK : (o + 1) * P * PACK, :]
            nc.sync.dma_start(w_raw[o][:], w_rows.rearrange("(p t) m -> p t m", t=PACK))
        load_words(1)
        with nc.allow_non_contiguous_dma(reason="one value a partition"):
            nc.sync.dma_start(thr_col[:], thr[0].rearrange("(j p) -> p j", p=P))
            nc.sync.dma_start(rated_col[:], rated[0].rearrange("(j p) -> p j", p=P))
        nc.sync.dma_start(geo_t[:], geo.rearrange("d p s -> p d s"))
        for d, pos in enumerate((pos1, pos2, pos3)):
            nc.sync.dma_start(pos_t[d][:], pos)
        nc.sync.dma_start(fat_row[:], fat.rearrange("m o -> (m o)").partition_broadcast(P))

        make_identity(nc, ident[:])
        for u in range(UNITS):
            nc.gpsimd.memset(windows[u][:, S:], 0.0)

        halves = [slice(0, JT // 2), slice(JT // 2, JT)]
        picked_planes = sb.tile([P, S], U8, name="picked_planes", align_bytes=64)
        expy = sb.tile([P, JT, UNITS, P], F32, name="expy")
        y = [ps.tile([P, JT // 2, N], F32, name=f"y{h}") for h in range(2)]

        def quantise(o, tag):
            grouped = sb.tile([P, N, PACK], BF16, name=f"grouped{o}", tag=tag, align_bytes=64)
            for u in range(UNITS):
                m_cols = slice(u * P, (u + 1) * P)
                dst = grouped[:, m_cols, :].rearrange("p (c i) t -> p c t i", i=4)
                src = w_raw[o][:, :, m_cols].rearrange("p t (c i) -> p c t i", i=4)
                if o == PASSES - 1 and u == UNITS - 1:
                    nc.vector.tensor_copy(dst, src)
                else:
                    nc.scalar.activation(dst, src, ACT.Copy)
            w_codes = sb.tile([P, N], U32, name=f"w_codes{o}", align_bytes=64)
            w_scales = sb.tile([P, N], U8, name=f"w_scales{o}", align_bytes=64)
            nc.vector.quantize_mx(
                out=w_codes[:].bitcast(FP8X4), scales=w_scales[:], in_=grouped[:].rearrange("p m t -> p (m t)")
            )
            return w_codes, w_scales

        def multiply(o, h, picked, w_codes, w_scales):
            for i in range(JT // 2):
                jt = halves[h].start + i
                cols = slice(jt * P, (jt + 1) * P)
                nc.tensor.matmul_mx(
                    out=y[h][:, i, :],
                    lhsT=picked[:, cols].bitcast(FP8X4),
                    lhsT_scale=picked_planes[4 * o : P, cols],
                    rhs=w_codes[:].bitcast(FP8X4),
                    rhs_scale=w_scales[:],
                    start=(o == 0 and i == 0),
                    stop=(o == PASSES - 1 and i == JT // 2 - 1),
                )

        picked0 = sb.tile([P, S], U32, name="picked0", align_bytes=64)
        nc.vector.tensor_copy(picked0[:], words[0][:].bitcast(U32).indirect(offs_t[:]))
        nc.vector.tensor_copy(picked_planes[:], planes[:].indirect(offs_t[:]))
        weights0 = quantise(0, "grouped0")
        for h in range(2):
            multiply(0, h, picked0, *weights0)
        weights1 = quantise(1, "grouped1_then_picked1")
        picked1 = sb.tile([P, S], U32, name="picked1", tag="grouped1_then_picked1", align_bytes=64)
        for h in range(2):
            nc.vector.tensor_copy(
                picked1[:, h * S // 2 : (h + 1) * S // 2],
                words[1][:].bitcast(U32).indirect(offs_t[:, h * S // 32 : (h + 1) * S // 32]),
            )
            multiply(1, h, picked1, *weights1)
            nc.scalar.activation(expy[:, halves[h]].rearrange("p j u m -> p j (u m)"), y[h][:], ACT.Exp)

        thr_part = sb.tile([P, JT], F32, name="thr_part")
        cap = sb.tile([P, JT], F32, name="cap")
        neg_rated = sb.tile([P, JT], F32, name="neg_rated")
        positive = sb.tile([P, JT], F32, name="positive")
        den_sign = sb.tile([P, JT], F32, name="den_sign")
        den_scale = sb.tile([P, JT], F32, name="den_scale", tag="grouped1_then_picked1", align_bytes=64)
        nc.gpsimd.tensor_scalar(thr_part[:], thr_col[:], THR_FLOOR, 1.0 / 0.3, ALU.add, ALU.mult)
        nc.gpsimd.tensor_scalar(cap[:], rated_col[:], 1.0 / CUBE, 0.0, ALU.mult, ALU.add)
        nc.gpsimd.tensor_scalar(neg_rated[:], rated_col[:], -1.0 / CUBE, 0.0, ALU.mult, ALU.add)
        nc.gpsimd.tensor_scalar(positive[:], rated_col[:], -0.1, None, ALU.is_ge)
        nc.gpsimd.tensor_scalar(den_sign[:], positive[:], 2.0, -1.0, ALU.mult, ALU.add)
        nc.vector.reciprocal(den_scale[:], thr_part[:])

        capped = sb.tile([P, JT, UNITS, P], F32, name="capped")
        log1p = sb.tile([P, JT, UNITS, P], F32, name="log1p")
        sp = sb.tile([P, JT, UNITS, P], F32, name="sp")
        nc.vector.tensor_scalar(capped[:], expy[:], EXP_CAP, None, ALU.min)
        geo_sq = sb.tile([P, D, S], F32, name="geo_sq", tag="words1", align_bytes=64)
        for d in range(D):
            nc.vector.tensor_tensor(geo_sq[:, d, :], geo_t[:, d, :], geo_t[:, d, :], ALU.mult)
        for h in halves:
            nc.scalar.activation(log1p[:, h], capped[:, h], ACT.Ln, bias=math.exp(SHIFT), scale=math.exp(SHIFT))
        den = sb.tile([P, JT, UNITS, P], F32, name="den")
        for h in range(2):
            nc.vector.scalar_tensor_tensor(
                sp[:, halves[h]].rearrange("p j u m -> p j (u m)"), y[h][:], SHIFT,
                log1p[:, halves[h]].rearrange("p j u m -> p j (u m)"), ALU.add, ALU.max,
            )
            for jt in range(halves[h].start, halves[h].stop):
                nc.vector.tensor_scalar(den[:, jt], sp[:, jt], 2.0, den_scale[:, jt : jt + 1], ALU.add, ALU.mult)
        quad = sb.tile([P, JT, UNITS, P], F32, name="quad")
        cubic = sb.tile([P, JT, UNITS, P], F32, name="cubic")
        for h in halves:
            nc.vector.tensor_tensor(quad[:, h], sp[:, h], sp[:, h], ALU.mult)
        for h in halves:
            nc.vector.tensor_tensor(cubic[:, h], quad[:, h], sp[:, h], ALU.mult)
        power_den = sb.tile([P, JT, UNITS, P], F32, name="power_den")
        for jt in range(JT):
            nc.vector.tensor_scalar(
                power_den[:, jt], cubic[:, jt], cap[:, jt : jt + 1], 0.1 / CUBE, ALU.min, ALU.add
            )
        shared = power_den[:].rearrange("p j u m -> p (j u m)")

        inv_root = sb.tile([P, JT, UNITS, P], F32, name="inv_root")
        ctas = [inv_root[:].rearrange("p j u m -> p (j u m)")[:, 0:S], shared[:, 0:S]]
        root_T = []
        for u in range(UNITS):
            root = sb.tile([P, JT, P], F32, name=f"root{u}")
            root_ps = ps.tile([P, JT, P], F32, name=f"root_ps{u}")
            nc.scalar.activation(root[:], den[:, :, u, :], ACT.Abs_reciprocal_sqrt)
            for jt in range(JT):
                nc.tensor.transpose(root_ps[:, jt, :], root[:, jt, :], ident[:])
            root_T.append(root_ps)
        for u in range(UNITS):
            if u == UNITS - 1:
                nc.scalar.activation(inv_root[:], power_den[:], ACT.Abs_reciprocal_sqrt)
            nc.scalar.activation(ctas[u], root_T[u][:].rearrange("p j m -> p (j m)"), ACT.Square)
            nc.scalar.activation(windows[u][:, 0:S], ctas[u], ACT.Square)

        s_T = []
        for u in range(UNITS):
            s_u = ps.tile([P, JT, P], F32, name=f"s_T{u}")
            for d in range(D):
                term = sb.tile([P, S], F32, name=f"term{u}{d}")
                nc.vector.tensor_tensor(term[:], windows[u][:].indirect(pos_t[d][:]), geo_sq[:, d, :], ALU.mult)
                for jt in range(JT):
                    nc.tensor.matmul(
                        s_u[:, jt, :], term[:, jt * P : (jt + 1) * P], ident[:],
                        start=(d == 0 and jt == 0), stop=(d == D - 1 and jt == JT - 1), is_transpose=True,
                    )
            s_T.append(s_u)

        inv_abs = [sb.tile([P, JT, P], F32, name=f"inv_abs{u}") for u in range(UNITS)]
        inv = sb.tile([P, JT, UNITS, P], F32, name="inv")
        chunks = [(0, slice(0, JT), "out0"), (1, halves[0], "y0"), (1, halves[1], "y1")]
        deficit = []
        kept_sq = []
        loss = []
        for u in range(UNITS):
            m_cols = slice(u * P, (u + 1) * P)
            deficit_u = shared[:, 0:S] if u == 0 else inv_abs[0][:].rearrange("p j m -> p (j m)")
            nc.scalar.activation(deficit_u, s_T[u][:].rearrange("p j m -> p (j m)"), ACT.Sqrt, bias=0.0004)
            kept_u = sb.tile([P, JT, P], F32, name=f"kept_sq{u}")
            nc.scalar.activation(kept_u[:].rearrange("p j m -> p (j m)"), deficit_u, ACT.Square, bias=1.0, scale=-1.0)
            nc.scalar.activation(inv_abs[u][:], inv_root[:, :, u, :], ACT.Square)
            for jt in range(JT):
                nc.scalar.activation(inv[:, jt, u, :], inv_abs[u][:, jt, :], ACT.Copy, scale=den_sign[:, jt : jt + 1])
            loss_u = sb.tile([P, JT, P], F32, name=f"loss{u}")
            nc.vector.scalar_tensor_tensor(
                loss_u[:], s_T[u][:], 0.0004, fat_row[:, m_cols].unsqueeze(1).to_broadcast([P, JT, P]), ALU.add, ALU.mult
            )
            deficit.append(deficit_u.rearrange("p (j m) -> p j m", m=P))
            kept_sq.append(kept_u)
            loss.append(loss_u)
        for c, (u, js, tag) in enumerate(chunks):
            n_j = js.stop - js.start
            neg_kept3 = sb.tile([P, n_j, P], F32, name=f"neg_kept3{c}")
            nc.vector.scalar_tensor_tensor(
                neg_kept3[:], deficit[u][:, js, :], 1.0, kept_sq[u][:, js, :], ALU.subtract, ALU.mult
            )
            neg_ua3 = sb.tile([P, n_j, P], F32, name=f"neg_ua3{c}")
            nc.vector.tensor_tensor(neg_ua3[:], cubic[:, js, u, :], neg_kept3[:], ALU.mult)
            neg_eff = sb.tile([P, n_j, P], F32, name=f"neg_eff{c}")
            out_ps = ps.tile([P, n_j, P], F32, name=f"out_ps{c}", tag=tag)
            for i in range(n_j):
                jt = js.start + i
                nc.tensor.matmul(
                    out_ps[:, i, :], loss[u][:, jt, :], ident[:], start=(i == 0), stop=False, is_transpose=True
                )
            for i in range(n_j):
                jt = js.start + i
                nc.vector.scalar_tensor_tensor(
                    neg_eff[:, i, :], neg_ua3[:, i, :], neg_rated[:, jt : jt + 1], inv[:, jt, u, :], ALU.max, ALU.mult
                )
                nc.tensor.matmul(
                    out_ps[:, i, :], neg_eff[:, i, :], ident[:], start=False, stop=(i == n_j - 1), is_transpose=True
                )
            result = sb.tile([P, n_j * P], F32, name=f"result{c}")
            nc.scalar.activation(result[:], out_ps[:].rearrange("p j m -> p (j m)"), ACT.Copy, scale=-1.0)
            queue = nc.scalar if c == len(chunks) - 1 else nc.sync
            queue.dma_start(out[u * P : (u + 1) * P, js.start * P : js.stop * P], result[:])
